import numpy as np, ml_dtypes
CORES = [122,123,126,250,251,254,378,379,382,506,507,510]
N = 12
import mx_ref
NC, KB = 128, 1
BF = ml_dtypes.bfloat16
def cut(t, i, w=512):
    return t[:, w * i:w * i + w]
def term(a, B):
    return np.stack([mx_ref.matmul(mx_ref.quantize(cut(a, i)), B) for i in range(4)], axis=2).reshape(128, -1)
def setup_inputs(rng):
    def f(*shape):
        return mx_ref.flush((rng.standard_normal(shape, dtype=np.float32) * np.exp2(rng.integers(-2, 3, shape[:-1] + (1,)))).astype(BF))
    return {"a": f(N, 128, 4 * 512), "b": f(N, 128, KB * 4 * NC)}
def setup_inputs_blocks(rng):
    d = setup_inputs(rng)
    for k in ("a", "b"): d[k] = mx_ref.spread(d[k], rng, 2)
    return d
def setup_inputs_wide(rng):
    d = setup_inputs(rng)
    for k in ("a", "b"): d[k] = mx_ref.flush((d[k].astype(np.float32) * np.exp2(rng.integers(-4, 5, (N, 1, 1))).astype(np.float32)).astype(BF))
    return d
def setup_inputs_lossless(rng):
    a = np.zeros((N, 128, 4 * 128, 4), np.float32)
    for r in range(N):
        k = rng.integers(0, 512, size=4 * 128)
        a[r, k // 4, np.arange(4 * 128), k % 4] = 1.0
    size = np.repeat(2.0 ** rng.integers(-4, 5, size=(1, 1, (KB * 4 * NC) // 4)), 4, axis=2)
    b = rng.integers(-1, 2, size=(N, 128, KB * 4 * NC)) * size
    return {"a": a.reshape(N, 128, 4 * 512).astype(BF), "b": b.astype(np.float32).astype(BF)}
def reference(a, b):
    y = np.zeros((N, 128, KB * 4 * NC), np.float32)
    for k in range(KB):
        y[:, :, 4 * NC * k:4 * NC * k + 4 * NC] = mx_ref.total([term(a[r], mx_ref.quantize(cut(b[r], k, 4 * NC))) for r in range(N)])
    return {"y": y}

@@ -1,0 +1,189 @@
+from concourse.bass import DstId, RemoteDMATransfer
+from concourse.mybir import dt, AluOpType, ActivationFunctionType
+
+_C, _P, _B = "float8_e4m3fn_x4", "uint8", "bfloat16"
+SCRATCH = {
+    "a_sb": ("sbuf", [128, 2048], _B), "b_sb": ("sbuf", [128, 512], _B),
+    "ones": ("sbuf", [128, 516], _B), "e_sb": ("sbuf", [128, 516], _B),
+    "qa": ("sbuf", [128, 512], _C), "sa": ("sbuf", [128, 512], _P),
+    "qb": ("sbuf", [128, 128], _C), "sb": ("sbuf", [128, 128], _P),
+    "qw": ("sbuf", [128, 512], _C), "sw": ("sbuf", [128, 512], _P),
+    "tst": ("sbuf", [128, 512], _B), "qt": ("sbuf", [128, 128], _C), "pt": ("sbuf", [128, 128], _P),
+    "hst": ("sbuf", [128, 512], _B), "qh": ("sbuf", [128, 128], _C), "ph": ("sbuf", [128, 128], _P),
+    "yst": ("sbuf", [128, 512], "float32"),
+    "ps": ("psum", [128, 4096], "float32"),
+}
+_LAND = ["t0", "t1", "t2", "gm", "gp", "gd"]
+for _n in _LAND:
+    SCRATCH[_n + "c"] = ("sbuf", [128, 128], _C)
+    SCRATCH[_n + "p"] = ("sbuf", [128, 128], _P)
+
+SEMAPHORES = (["ones", "esel", "qw", "lb", "la", "la3", "qb", "tc", "qt", "hc", "qh", "yc", "st", "sent"]
+              + ["qa%d" % i for i in range(4)] + ["mm%d" % i for i in range(4)]
+              + ["hm%d" % i for i in range(4)] + ["fm%d" % i for i in range(4)]
+              + [n + k for n in _LAND for k in "cp"])
+
+
+def _plan(T, topo):
+    cores = list(T.cores)
+    hosts = sorted(set(topo.host(c) for c in cores))
+    mine = dict((h, [c for c in cores if topo.host(c) == h]) for h in hosts)
+    ring = [hosts[0]]
+    while len(ring) < len(hosts):
+        ring.append([h for h in hosts if h not in ring and topo.may_write(mine[ring[-1]][0], mine[h][0])][0])
+    roles = {}
+    for h in hosts:
+        pair = [c for c in mine[h] if len([d for d in mine[h] if topo.die(d) == topo.die(c)]) == 2]
+        lone = [c for c in mine[h] if c not in pair]
+        roles[h] = (pair[0], pair[1], lone[0])
+    return ring, mine, roles
+
+
+def rank_program(g, core, T, topo):
+    if T.rank_of(core) is None:
+        return
+    S = T.sem
+    ring, mine, roles = _plan(T, topo)
+    h = topo.host(core)
+    k = ring.index(h)
+    fwd, back = ring[(k + 1) % len(ring)], ring[(k - 1) % len(ring)]
+    X, R, Z = roles[h]
+    me = mine[h].index(core)
+    others = [c for c in mine[h] if c != core]
+    full = topo.mask(core, others[0])
+    lo = full & topo.mask(core, roles[fwd][0])
+    hi = full & ~lo
+    sent = [0]
+
+    def bits(m):
+        return bin(m).count("1")
+
+    def view(name):
+        return T[name][:].bitcast(dt.uint8) if name.endswith("c") or name in ("qt", "qh") else T[name][:]
+
+    def send(dst, land, src, mask):
+        rid, pid = topo.addr(dst, core)
+        g.remote_dma(view(land), view(src), S[land], S.sent, pid, rid, mask)
+        sent[0] += bits(mask)
+
+    def spread(name):
+        tr = []
+        for dst, m in zip(others, (lo, hi)):
+            rid, pid = topo.addr(dst, core)
+            tr.append(RemoteDMATransfer(dst_ids=[DstId(rid=rid, pnc=pid)], dma_engine_mask=m, remote_sem=S[name],
+                                        src=view(name), dst=view(name)))
+            sent[0] += bits(m)
+        g.remote_dma_fused(tr, local_sem=S.sent)
+
+    n_in = bits(lo)
+    bank = [T.ps[:, 512 * b:512 * b + 128] for b in range(8)]
+    low, high = bank[0:4], bank[4:8]
+    col = lambda t, b: t[:, 128 * b:128 * b + 128]
+
+    def product(out, i, stop):
+        return g.tensor.matmul_mx(out, col(T.qa, i), col(T.sa, i), T.qb[:], T.sb[:], True, stop)
+
+    g.sync.dma_start(T.a_sb[:, 0:1536], T.a[:, 0:1536]).then_inc(S.la, 16)
+    g.scalar.dma_start(T.b_sb[:], T.b[:]).then_inc(S.lb, 16)
+    g.sync.dma_start(T.a_sb[:, 1536:2048], T.a[:, 1536:2048]).then_inc(S.la3, 16)
+
+    g.vector.memset(T.ones[:], 1.0).then_inc(S.ones, 1)
+    g.wait_ge(S.ones, 1)
+    g.affine_select(T.e_sb[:], T.ones[:], [[-1, 516]], AluOpType.is_equal, 0.0, 3, 4).then_inc(S.esel, 1)
+    g.vector.wait_ge(S.esel, 1)
+    for b in range(4):
+        g.vector.quantize_mx(col(T.qw, b), col(T.sw, b), T.e_sb[:, 3 - b:3 - b + 512]).then_inc(S.qw, 1)
+
+    g.vector.wait_ge(S.lb, 16)
+    g.vector.quantize_mx(T.qb[:], T.sb[:], T.b_sb[:]).then_inc(S.qb, 1)
+    g.tensor.wait_ge(S.qb, 1)
+    for i in range(4):
+        g.vector.wait_ge(S.la if i < 3 else S.la3, 16)
+        g.vector.quantize_mx(col(T.qa, i), col(T.sa, i), T.a_sb[:, 512 * i:512 * i + 512]).then_inc(S["qa%d" % i], 1)
+        g.tensor.wait_ge(S["qa%d" % i], 1)
+        product(low[i], i, True).then_inc(S["mm%d" % i], 1)
+        g.scalar.wait_ge(S["mm%d" % i], 1)
+        g.scalar.activation(T.tst[:, i:512:4], low[i], ActivationFunctionType.Copy).then_inc(S.tc, 1)
+    g.vector.wait_ge(S.tc, 4)
+    g.vector.quantize_mx(T.qt[:], T.pt[:], T.tst[:]).then_inc(S.qt, 1)
+
+    first = {X: Z, R: X, Z: X}
+    g.wait_ge(S.qt, 1)
+    for dst in [first[core]] + [c for c in others if c != first[core]]:
+        send(dst, "t%dc" % me, "qt", lo)
+        send(dst, "t%dp" % me, "pt", hi)
+
+    def add(name, banks, last_sem=None):
+        g.tensor.wait_ge(S[name + "c"], n_in)
+        g.tensor.wait_ge(S[name + "p"], n_in)
+        for b in range(4):
+            mm = g.tensor.matmul_mx(banks[b], col(T.qw, b), col(T.sw, b), T[name + "c"][:], T[name + "p"][:],
+                                    False, last_sem is not None)
+            if last_sem:
+                mm.then_inc(S["%s%d" % (last_sem, b)], 1)
+
+    def drain(tile, banks, sem_in, sem_out):
+        for b in range(4):
+            if b % 2 == 0:
+                g.scalar.wait_ge(S["%s%d" % (sem_in, b)], 1)
+                g.scalar.activation(tile[:, b:512:4], banks[b], ActivationFunctionType.Copy).then_inc(S[sem_out], 1)
+            else:
+                g.vector.wait_ge(S["%s%d" % (sem_in, b)], 1)
+                g.vector.tensor_copy(tile[:, b:512:4], banks[b]).then_inc(S[sem_out], 1)
+
+    peers = ["t%d" % mine[h].index(c)
+             for c in ([c for c in others if first[c] == core] + [c for c in others if first[c] != core])]
+    for i in range(4):
+        product(high[i], i, False)
+    g.tensor.wait_ge(S.qw, 4)
+    if core == R:
+        final = high
+        add(peers[0], final)
+        add(peers[1], final)
+        g.tensor.wait_ge(S.tc, 4)
+    else:
+        add(peers[0], high)
+        add(peers[1], high, "hm")
+        drain(T.hst, high, "hm", "hc")
+        g.vector.wait_ge(S.hc, 4)
+        g.vector.quantize_mx(T.qh[:], T.ph[:], T.hst[:]).then_inc(S.qh, 1)
+        g.wait_ge(S.qh, 1)
+        if core == X:
+            send(roles[fwd][1], "gmc", "qh", lo)
+            send(roles[fwd][0], "gmp", "ph", lo)
+        else:
+            send(roles[back][2], "gpc", "qh", lo)
+            send(roles[back][0], "gpp", "ph", lo)
+        final = low
+        g.tensor.wait_ge(S.tc, 4)
+        for i in range(4):
+            product(final[i], i, False)
+        add(peers[0], final)
+        add(peers[1], final)
+
+    if core == R:
+        g.wait_ge(S.gmc, n_in)
+        send(roles[fwd][2], "gdc", "gmc", lo)
+        spread("gmc")
+    if core == X:
+        g.wait_ge(S.gmp, n_in)
+        send(roles[fwd][0], "gdp", "gmp", lo)
+        spread("gmp")
+        g.wait_ge(S.gpp, n_in)
+        spread("gpp")
+        g.wait_ge(S.gdp, n_in)
+        spread("gdp")
+    if core == Z:
+        g.wait_ge(S.gpc, n_in)
+        spread("gpc")
+        g.wait_ge(S.gdc, n_in)
+        spread("gdc")
+
+    add("gm", final)
+    add("gp", final)
+    add("gd", final, "fm")
+    drain(T.yst, final, "fm", "yc")
+    g.sync.wait_ge(S.yc, 4)
+    g.sync.dma_start(T.y[:], T.yst[:]).then_inc(S.st, 16)
+    g.sync.wait_ge(S.st, 16)
+    g.wait_ge(S.sent, sent[0])

@@ -7,18 +7,16 @@ SCRATCH = {
     "ones": ("sbuf", [128, 516], _B), "e_sb": ("sbuf", [128, 516], _B),
     "qa": ("sbuf", [128, 512], _C), "sa": ("sbuf", [128, 512], _P),
     "qb": ("sbuf", [128, 128], _C), "sb": ("sbuf", [128, 128], _P),
-    "qw": ("sbuf", [128, 512], _C), "sw": ("sbuf", [128, 512], _P),
-    "tst": ("sbuf", [128, 512], _B), "qt": ("sbuf", [128, 128], _C), "pt": ("sbuf", [128, 128], _P),
-    "hst": ("sbuf", [128, 512], _B), "qh": ("sbuf", [128, 128], _C), "ph": ("sbuf", [128, 128], _P),
+    "tst": ("sbuf", [128, 512], _B), "hst": ("sbuf", [128, 512], _B),
     "yst": ("sbuf", [128, 512], "float32"),
     "ps": ("psum", [128, 4096], "float32"),
 }
-_LAND = ["t0", "t1", "t2", "gm", "gp", "gd"]
-for _n in _LAND:
+_LAND = ["w0", "w1", "w2", "t0", "t1", "t2", "gm", "gp", "gd"]
+for _n in _LAND + ["w3", "ot", "oh"]:
     SCRATCH[_n + "c"] = ("sbuf", [128, 128], _C)
     SCRATCH[_n + "p"] = ("sbuf", [128, 128], _P)
 
-SEMAPHORES = (["ones", "esel", "qw", "lb", "la", "la3", "qb", "tc", "qt", "hc", "qh", "yc", "st", "sent"]
+SEMAPHORES = (["ones", "esel", "qw", "qw3", "lb", "la", "la3", "qb", "tc", "qt", "hc", "qh", "yc", "st", "sent"]
               + ["qa%d" % i for i in range(4)] + ["mm%d" % i for i in range(4)]
               + ["hm%d" % i for i in range(4)] + ["fm%d" % i for i in range(4)]
               + [n + k for n in _LAND for k in "cp"])
@@ -59,7 +57,7 @@ def rank_program(g, core, T, topo):
         return bin(m).count("1")
 
     def view(name):
-        return T[name][:].bitcast(dt.uint8) if name.endswith("c") or name in ("qt", "qh") else T[name][:]
+        return T[name][:].bitcast(dt.uint8) if name.endswith("c") else T[name][:]
 
     def send(dst, land, src, mask):
         rid, pid = topo.addr(dst, core)
@@ -91,8 +89,11 @@ def rank_program(g, core, T, topo):
     g.wait_ge(S.ones, 1)
     g.affine_select(T.e_sb[:], T.ones[:], [[-1, 516]], AluOpType.is_equal, 0.0, 3, 4).then_inc(S.esel, 1)
     g.vector.wait_ge(S.esel, 1)
-    for b in range(4):
-        g.vector.quantize_mx(col(T.qw, b), col(T.sw, b), T.e_sb[:, 3 - b:3 - b + 512]).then_inc(S.qw, 1)
+    g.vector.quantize_mx(T["w%dc" % me][:], T["w%dp" % me][:], T.e_sb[:, 3 - me:3 - me + 512]).then_inc(S.qw, 1)
+    g.vector.quantize_mx(T.w3c[:], T.w3p[:], T.e_sb[:, 0:512]).then_inc(S.qw3, 1)
+    g.wait_ge(S.qw, 1)
+    spread("w%dc" % me)
+    spread("w%dp" % me)
 
     g.vector.wait_ge(S.lb, 16)
     g.vector.quantize_mx(T.qb[:], T.sb[:], T.b_sb[:]).then_inc(S.qb, 1)
@@ -105,19 +106,19 @@ def rank_program(g, core, T, topo):
         g.scalar.wait_ge(S["mm%d" % i], 1)
         g.scalar.activation(T.tst[:, i:512:4], low[i], ActivationFunctionType.Copy).then_inc(S.tc, 1)
     g.vector.wait_ge(S.tc, 4)
-    g.vector.quantize_mx(T.qt[:], T.pt[:], T.tst[:]).then_inc(S.qt, 1)
+    g.vector.quantize_mx(T.otc[:], T.otp[:], T.tst[:]).then_inc(S.qt, 1)
 
     first = {X: Z, R: X, Z: X}
     g.wait_ge(S.qt, 1)
     for dst in [first[core]] + [c for c in others if c != first[core]]:
-        send(dst, "t%dc" % me, "qt", lo)
-        send(dst, "t%dp" % me, "pt", hi)
+        send(dst, "t%dc" % me, "otc", lo)
+        send(dst, "t%dp" % me, "otp", hi)
 
     def add(name, banks, last_sem=None):
         g.tensor.wait_ge(S[name + "c"], n_in)
         g.tensor.wait_ge(S[name + "p"], n_in)
         for b in range(4):
-            mm = g.tensor.matmul_mx(banks[b], col(T.qw, b), col(T.sw, b), T[name + "c"][:], T[name + "p"][:],
+            mm = g.tensor.matmul_mx(banks[b], T["w%dc" % b][:], T["w%dp" % b][:], T[name + "c"][:], T[name + "p"][:],
                                     False, last_sem is not None)
             if last_sem:
                 mm.then_inc(S["%s%d" % (last_sem, b)], 1)
@@ -135,7 +136,11 @@ def rank_program(g, core, T, topo):
              for c in ([c for c in others if first[c] == core] + [c for c in others if first[c] != core])]
     for i in range(4):
         product(high[i], i, False)
-    g.tensor.wait_ge(S.qw, 4)
+    g.tensor.wait_ge(S.qw, 1)
+    g.tensor.wait_ge(S.qw3, 1)
+    for c in others:
+        g.tensor.wait_ge(S["w%dc" % mine[h].index(c)], n_in)
+        g.tensor.wait_ge(S["w%dp" % mine[h].index(c)], n_in)
     if core == R:
         final = high
         add(peers[0], final)
@@ -146,14 +151,14 @@ def rank_program(g, core, T, topo):
         add(peers[1], high, "hm")
         drain(T.hst, high, "hm", "hc")
         g.vector.wait_ge(S.hc, 4)
-        g.vector.quantize_mx(T.qh[:], T.ph[:], T.hst[:]).then_inc(S.qh, 1)
+        g.vector.quantize_mx(T.ohc[:], T.ohp[:], T.hst[:]).then_inc(S.qh, 1)
         g.wait_ge(S.qh, 1)
         if core == X:
-            send(roles[fwd][1], "gmc", "qh", lo)
-            send(roles[fwd][0], "gmp", "ph", lo)
+            send(roles[fwd][1], "gmc", "ohc", lo)
+            send(roles[fwd][0], "gmp", "ohp", lo)
         else:
-            send(roles[back][2], "gpc", "qh", lo)
-            send(roles[back][0], "gpp", "ph", lo)
+            send(roles[back][2], "gpc", "ohc", lo)
+            send(roles[back][0], "gpp", "ohp", lo)
         final = low
         g.tensor.wait_ge(S.tc, 4)
         for i in range(4):

@@ -11,15 +11,15 @@ SCRATCH = {
     "yst": ("sbuf", [128, 512], "float32"),
     "ps": ("psum", [128, 4096], "float32"),
 }
-_LAND = ["w0", "w1", "w2", "t0", "t1", "t2", "gm", "gp", "gd"]
-for _n in _LAND + ["w3", "ot", "oh"]:
+_PARTS = {"w0": "cp", "w1": "cp", "w2": "cp", "t0": "cp", "t1": "cp", "t2": "cp", "gm": "abp", "gp": "cp", "gd": "abp"}
+for _n in list(_PARTS) + ["w3", "ot", "oh"]:
     SCRATCH[_n + "c"] = ("sbuf", [128, 128], _C)
     SCRATCH[_n + "p"] = ("sbuf", [128, 128], _P)
 
-SEMAPHORES = (["ones", "esel", "qw", "qw3", "lb", "la", "la3", "qb", "tc", "qt", "hc", "qh", "yc", "st", "sent"]
+SEMAPHORES = (["ones", "esel", "qw", "qw3", "lb", "la", "la3", "qb", "tc", "qt", "hc", "qh", "yc", "st", "sent", "gmq", "gmr"]
               + ["qa%d" % i for i in range(4)] + ["mm%d" % i for i in range(4)]
               + ["hm%d" % i for i in range(4)] + ["fm%d" % i for i in range(4)]
-              + [n + k for n in _LAND for k in "cp"])
+              + [n + k for n in _PARTS for k in _PARTS[n]])
 
 
 def _plan(T, topo):
@@ -46,6 +46,7 @@ def rank_program(g, core, T, topo):
     k = ring.index(h)
     fwd, back = ring[(k + 1) % len(ring)], ring[(k - 1) % len(ring)]
     X, R, Z = roles[h]
+    nr = len(mine[h])
     me = mine[h].index(core)
     others = [c for c in mine[h] if c != core]
     full = topo.mask(core, others[0])
@@ -56,24 +57,28 @@ def rank_program(g, core, T, topo):
     def bits(m):
         return bin(m).count("1")
 
-    def view(name):
-        return T[name][:].bitcast(dt.uint8) if name.endswith("c") else T[name][:]
+    count = {"w": bits(full), "t": bits(full), "g": bits(lo)}
 
-    def send(dst, land, src, mask):
+    def view(tile, part):
+        t = T[tile + ("p" if part in "pqr" else "c")]
+        half = t.shape[1] // 2
+        v = t[:, 0:half] if part in "aq" else t[:, half:2 * half] if part in "br" else t[:]
+        return v if part in "pqr" else v.bitcast(dt.uint8)
+
+    def send(dst, land, src, part, mask):
         rid, pid = topo.addr(dst, core)
-        g.remote_dma(view(land), view(src), S[land], S.sent, pid, rid, mask)
+        g.remote_dma(view(land, part), view(src, part), S[land + part], S.sent, pid, rid, mask)
         sent[0] += bits(mask)
 
-    def spread(name):
+    def spread(tile, part):
         tr = []
         for dst, m in zip(others, (lo, hi)):
             rid, pid = topo.addr(dst, core)
-            tr.append(RemoteDMATransfer(dst_ids=[DstId(rid=rid, pnc=pid)], dma_engine_mask=m, remote_sem=S[name],
-                                        src=view(name), dst=view(name)))
+            tr.append(RemoteDMATransfer(dst_ids=[DstId(rid=rid, pnc=pid)], dma_engine_mask=m, remote_sem=S[tile + part],
+                                        src=view(tile, part), dst=view(tile, part)))
             sent[0] += bits(m)
         g.remote_dma_fused(tr, local_sem=S.sent)
 
-    n_in = bits(lo)
     bank = [T.ps[:, 512 * b:512 * b + 128] for b in range(8)]
     low, high = bank[0:4], bank[4:8]
     col = lambda t, b: t[:, 128 * b:128 * b + 128]
@@ -85,15 +90,19 @@ def rank_program(g, core, T, topo):
     g.scalar.dma_start(T.b_sb[:], T.b[:]).then_inc(S.lb, 16)
     g.sync.dma_start(T.a_sb[:, 1536:2048], T.a[:, 1536:2048]).then_inc(S.la3, 16)
 
+    def select(s, sem):
+        g.vector.quantize_mx(T["w%dc" % s][:], T["w%dp" % s][:], T.e_sb[:, 3 - s:3 - s + 512]).then_inc(S[sem], 1)
+
     g.vector.memset(T.ones[:], 1.0).then_inc(S.ones, 1)
     g.wait_ge(S.ones, 1)
     g.affine_select(T.e_sb[:], T.ones[:], [[-1, 516]], AluOpType.is_equal, 0.0, 3, 4).then_inc(S.esel, 1)
     g.vector.wait_ge(S.esel, 1)
-    g.vector.quantize_mx(T["w%dc" % me][:], T["w%dp" % me][:], T.e_sb[:, 3 - me:3 - me + 512]).then_inc(S.qw, 1)
-    g.vector.quantize_mx(T.w3c[:], T.w3p[:], T.e_sb[:, 0:512]).then_inc(S.qw3, 1)
+    select(me, "qw")
+    select((me + 1) % nr, "qw3")
+    select(3, "qw3")
     g.wait_ge(S.qw, 1)
-    spread("w%dc" % me)
-    spread("w%dp" % me)
+    send(mine[h][(me + 1) % nr], "w%d" % me, "w%d" % me, "c", full)
+    send(mine[h][(me + 1) % nr], "w%d" % me, "w%d" % me, "p", full)
 
     g.vector.wait_ge(S.lb, 16)
     g.vector.quantize_mx(T.qb[:], T.sb[:], T.b_sb[:]).then_inc(S.qb, 1)
@@ -111,12 +120,12 @@ def rank_program(g, core, T, topo):
     first = {X: Z, R: X, Z: X}
     g.wait_ge(S.qt, 1)
     for dst in [first[core]] + [c for c in others if c != first[core]]:
-        send(dst, "t%dc" % me, "otc", lo)
-        send(dst, "t%dp" % me, "otp", hi)
+        send(dst, "t%d" % me, "ot", "c", full)
+        send(dst, "t%d" % me, "ot", "p", full)
 
     def add(name, banks, last_sem=None):
-        g.tensor.wait_ge(S[name + "c"], n_in)
-        g.tensor.wait_ge(S[name + "p"], n_in)
+        for part in ("abqr" if name == "gm" and core == X else _PARTS[name]):
+            g.tensor.wait_ge(S[name + part], count[name[0]])
         for b in range(4):
             mm = g.tensor.matmul_mx(banks[b], T["w%dc" % b][:], T["w%dp" % b][:], T[name + "c"][:], T[name + "p"][:],
                                     False, last_sem is not None)
@@ -132,57 +141,48 @@ def rank_program(g, core, T, topo):
                 g.vector.wait_ge(S["%s%d" % (sem_in, b)], 1)
                 g.vector.tensor_copy(tile[:, b:512:4], banks[b]).then_inc(S[sem_out], 1)
 
-    peers = ["t%d" % mine[h].index(c)
-             for c in ([c for c in others if first[c] == core] + [c for c in others if first[c] != core])]
+    term = lambda c: "t%d" % mine[h].index(c)
+    peers = {X: [term(R), term(Z)], Z: [term(X), term(R)], R: [term(X), term(Z)]}[core]
     for i in range(4):
         product(high[i], i, False)
     g.tensor.wait_ge(S.qw, 1)
-    g.tensor.wait_ge(S.qw3, 1)
-    for c in others:
-        g.tensor.wait_ge(S["w%dc" % mine[h].index(c)], n_in)
-        g.tensor.wait_ge(S["w%dp" % mine[h].index(c)], n_in)
-    if core == R:
-        final = high
-        add(peers[0], final)
-        add(peers[1], final)
-        g.tensor.wait_ge(S.tc, 4)
-    else:
-        add(peers[0], high)
-        add(peers[1], high, "hm")
-        drain(T.hst, high, "hm", "hc")
-        g.vector.wait_ge(S.hc, 4)
-        g.vector.quantize_mx(T.ohc[:], T.ohp[:], T.hst[:]).then_inc(S.qh, 1)
-        g.wait_ge(S.qh, 1)
-        if core == X:
-            send(roles[fwd][1], "gmc", "ohc", lo)
-            send(roles[fwd][0], "gmp", "ohp", lo)
-        else:
-            send(roles[back][2], "gpc", "ohc", lo)
-            send(roles[back][0], "gpp", "ohp", lo)
-        final = low
-        g.tensor.wait_ge(S.tc, 4)
-        for i in range(4):
-            product(final[i], i, False)
-        add(peers[0], final)
-        add(peers[1], final)
+    g.tensor.wait_ge(S.qw3, 2)
+    for part in "cp":
+        g.tensor.wait_ge(S["w%d%s" % ((me + nr - 1) % nr, part)], count["w"])
+    add(peers[0], high)
+    add(peers[1], high, "hm")
+    drain(T.hst, high, "hm", "hc")
+    g.vector.wait_ge(S.hc, 4)
+    g.vector.quantize_mx(T.ohc[:], T.ohp[:], T.hst[:]).then_inc(S.qh, 1)
 
-    if core == R:
-        g.wait_ge(S.gmc, n_in)
-        send(roles[fwd][2], "gdc", "gmc", lo)
-        spread("gmc")
+    g.wait_ge(S.qh, 1)
     if core == X:
-        g.wait_ge(S.gmp, n_in)
-        send(roles[fwd][0], "gdp", "gmp", lo)
-        spread("gmp")
-        g.wait_ge(S.gpp, n_in)
-        spread("gpp")
-        g.wait_ge(S.gdp, n_in)
-        spread("gdp")
-    if core == Z:
-        g.wait_ge(S.gpc, n_in)
-        spread("gpc")
-        g.wait_ge(S.gdc, n_in)
-        spread("gdc")
+        send(roles[fwd][1], "gm", "oh", "a", lo)
+        send(roles[fwd][0], "gm", "oh", "q", lo)
+    elif core == Z:
+        send(roles[fwd][2], "gm", "oh", "b", lo)
+        send(roles[fwd][0], "gm", "oh", "r", lo)
+    else:
+        send(roles[back][2], "gp", "oh", "c", lo)
+        send(roles[back][1], "gp", "oh", "p", lo)
+    final = low
+    g.tensor.wait_ge(S.tc, 4)
+    for i in range(4):
+        product(final[i], i, False)
+    add(peers[0], final)
+    add(peers[1], final)
+
+    place = {X: 0, R: 1, Z: 2}[core]
+    mine_of = {X: ("p", None), R: ("a", "p"), Z: ("b", "c")}[core]
+    for part in ("qr" if core == X else mine_of[0]):
+        g.wait_ge(S["gm" + part], count["g"])
+    send(roles[fwd][place], "gd", "gm", mine_of[0], lo)
+    spread("gm", mine_of[0])
+    if mine_of[1]:
+        g.wait_ge(S["gp" + mine_of[1]], count["g"])
+        spread("gp", mine_of[1])
+    g.wait_ge(S["gd" + mine_of[0]], count["g"])
+    spread("gd", mine_of[0])
 
     add("gm", final)
     add("gp", final)

from concourse.bass import DstId, RemoteDMATransfer
from concourse.mybir import dt, AluOpType, ActivationFunctionType

_C, _P, _B = "float8_e4m3fn_x4", "uint8", "bfloat16"
SCRATCH = {
    "a_sb": ("sbuf", [128, 2048], _B), "b_sb": ("sbuf", [128, 512], _B),
    "ones": ("sbuf", [128, 516], _B), "e_sb": ("sbuf", [128, 516], _B),
    "qa": ("sbuf", [128, 512], _C), "sa": ("sbuf", [128, 512], _P),
    "qb": ("sbuf", [128, 128], _C), "sb": ("sbuf", [128, 128], _P),
    "tst": ("sbuf", [128, 512], _B), "hst": ("sbuf", [128, 512], _B),
    "yst": ("sbuf", [128, 512], "float32"),
    "ps": ("psum", [128, 4096], "float32"),
}
_PARTS = {"w0": "cp", "w1": "cp", "w2": "cp", "t0": "cp", "t1": "cp", "t2": "cp", "gm": "abp", "gp": "cp", "gd": "abp"}
for _n in list(_PARTS) + ["w3", "ot", "oh"]:
    SCRATCH[_n + "c"] = ("sbuf", [128, 128], _C)
    SCRATCH[_n + "p"] = ("sbuf", [128, 128], _P)

SEMAPHORES = (["ones", "esel", "qw", "qw3", "lb", "la", "la3", "qb", "tc", "qt", "hc", "qh", "yc", "st", "sent", "gmq", "gmr"]
              + ["qa%d" % i for i in range(4)] + ["mm%d" % i for i in range(4)]
              + ["hm%d" % i for i in range(4)] + ["fm%d" % i for i in range(4)]
              + [n + k for n in _PARTS for k in _PARTS[n]])


def _plan(T, topo):
    cores = list(T.cores)
    hosts = sorted(set(topo.host(c) for c in cores))
    mine = dict((h, [c for c in cores if topo.host(c) == h]) for h in hosts)
    ring = [hosts[0]]
    while len(ring) < len(hosts):
        ring.append([h for h in hosts if h not in ring and topo.may_write(mine[ring[-1]][0], mine[h][0])][0])
    roles = {}
    for h in hosts:
        pair = [c for c in mine[h] if len([d for d in mine[h] if topo.die(d) == topo.die(c)]) == 2]
        lone = [c for c in mine[h] if c not in pair]
        roles[h] = (pair[0], pair[1], lone[0])
    return ring, mine, roles


def rank_program(g, core, T, topo):
    if T.rank_of(core) is None:
        return
    S = T.sem
    ring, mine, roles = _plan(T, topo)
    h = topo.host(core)
    k = ring.index(h)
    fwd, back = ring[(k + 1) % len(ring)], ring[(k - 1) % len(ring)]
    X, R, Z = roles[h]
    nr = len(mine[h])
    me = mine[h].index(core)
    others = [c for c in mine[h] if c != core]
    full = topo.mask(core, others[0])
    lo = full & topo.mask(core, roles[fwd][0])
    hi = full & ~lo
    sent = [0]

    def bits(m):
        return bin(m).count("1")

    count = {"w": bits(full), "t": bits(full), "g": bits(lo)}

    def view(tile, part):
        t = T[tile + ("p" if part in "pqr" else "c")]
        half = t.shape[1] // 2
        v = t[:, 0:half] if part in "aq" else t[:, half:2 * half] if part in "br" else t[:]
        return v if part in "pqr" else v.bitcast(dt.uint8)

    def send(dst, land, src, part, mask):
        rid, pid = topo.addr(dst, core)
        g.remote_dma(view(land, part), view(src, part), S[land + part], S.sent, pid, rid, mask)
        sent[0] += bits(mask)

    def spread(tile, part):
        tr = []
        for dst, m in zip(others, (lo, hi)):
            rid, pid = topo.addr(dst, core)
            tr.append(RemoteDMATransfer(dst_ids=[DstId(rid=rid, pnc=pid)], dma_engine_mask=m, remote_sem=S[tile + part],
                                        src=view(tile, part), dst=view(tile, part)))
            sent[0] += bits(m)
        g.remote_dma_fused(tr, local_sem=S.sent)

    bank = [T.ps[:, 512 * b:512 * b + 128] for b in range(8)]
    low, high = bank[0:4], bank[4:8]
    col = lambda t, b: t[:, 128 * b:128 * b + 128]

    def product(out, i, stop):
        return g.tensor.matmul_mx(out, col(T.qa, i), col(T.sa, i), T.qb[:], T.sb[:], True, stop)

    g.sync.dma_start(T.a_sb[:, 0:1536], T.a[:, 0:1536]).then_inc(S.la, 16)
    g.scalar.dma_start(T.b_sb[:], T.b[:]).then_inc(S.lb, 16)
    g.sync.dma_start(T.a_sb[:, 1536:2048], T.a[:, 1536:2048]).then_inc(S.la3, 16)

    def select(s, sem):
        g.vector.quantize_mx(T["w%dc" % s][:], T["w%dp" % s][:], T.e_sb[:, 3 - s:3 - s + 512]).then_inc(S[sem], 1)

    g.vector.memset(T.ones[:], 1.0).then_inc(S.ones, 1)
    g.wait_ge(S.ones, 1)
    g.affine_select(T.e_sb[:], T.ones[:], [[-1, 516]], AluOpType.is_equal, 0.0, 3, 4).then_inc(S.esel, 1)
    g.vector.wait_ge(S.esel, 1)
    select(me, "qw")
    select((me + 1) % nr, "qw3")
    select(3, "qw3")
    g.wait_ge(S.qw, 1)
    send(mine[h][(me + 1) % nr], "w%d" % me, "w%d" % me, "c", full)
    send(mine[h][(me + 1) % nr], "w%d" % me, "w%d" % me, "p", full)

    g.vector.wait_ge(S.lb, 16)
    g.vector.quantize_mx(T.qb[:], T.sb[:], T.b_sb[:]).then_inc(S.qb, 1)
    g.tensor.wait_ge(S.qb, 1)
    for i in range(4):
        g.vector.wait_ge(S.la if i < 3 else S.la3, 16)
        g.vector.quantize_mx(col(T.qa, i), col(T.sa, i), T.a_sb[:, 512 * i:512 * i + 512]).then_inc(S["qa%d" % i], 1)
        g.tensor.wait_ge(S["qa%d" % i], 1)
        product(low[i], i, True).then_inc(S["mm%d" % i], 1)
        g.scalar.wait_ge(S["mm%d" % i], 1)
        g.scalar.activation(T.tst[:, i:512:4], low[i], ActivationFunctionType.Copy).then_inc(S.tc, 1)
    g.vector.wait_ge(S.tc, 4)
    g.vector.quantize_mx(T.otc[:], T.otp[:], T.tst[:]).then_inc(S.qt, 1)

    first = {X: Z, R: X, Z: X}
    g.wait_ge(S.qt, 1)
    for dst in [first[core]] + [c for c in others if c != first[core]]:
        send(dst, "t%d" % me, "ot", "c", full)
        send(dst, "t%d" % me, "ot", "p", full)

    def add(name, banks, last_sem=None):
        for part in ("abqr" if name == "gm" and core == X else _PARTS[name]):
            g.tensor.wait_ge(S[name + part], count[name[0]])
        for b in range(4):
            mm = g.tensor.matmul_mx(banks[b], T["w%dc" % b][:], T["w%dp" % b][:], T[name + "c"][:], T[name + "p"][:],
                                    False, last_sem is not None)
            if last_sem:
                mm.then_inc(S["%s%d" % (last_sem, b)], 1)

    def drain(tile, banks, sem_in, sem_out):
        for b in range(4):
            if b % 2 == 0:
                g.scalar.wait_ge(S["%s%d" % (sem_in, b)], 1)
                g.scalar.activation(tile[:, b:512:4], banks[b], ActivationFunctionType.Copy).then_inc(S[sem_out], 1)
            else:
                g.vector.wait_ge(S["%s%d" % (sem_in, b)], 1)
                g.vector.tensor_copy(tile[:, b:512:4], banks[b]).then_inc(S[sem_out], 1)

    term = lambda c: "t%d" % mine[h].index(c)
    peers = {X: [term(R), term(Z)], Z: [term(X), term(R)], R: [term(X), term(Z)]}[core]
    for i in range(4):
        product(high[i], i, False)
    g.tensor.wait_ge(S.qw, 1)
    g.tensor.wait_ge(S.qw3, 2)
    for part in "cp":
        g.tensor.wait_ge(S["w%d%s" % ((me + nr - 1) % nr, part)], count["w"])
    add(peers[0], high)
    add(peers[1], high, "hm")
    drain(T.hst, high, "hm", "hc")
    g.vector.wait_ge(S.hc, 4)
    g.vector.quantize_mx(T.ohc[:], T.ohp[:], T.hst[:]).then_inc(S.qh, 1)

    g.wait_ge(S.qh, 1)
    if core == X:
        send(roles[fwd][1], "gm", "oh", "a", lo)
        send(roles[fwd][0], "gm", "oh", "q", lo)
    elif core == Z:
        send(roles[fwd][2], "gm", "oh", "b", lo)
        send(roles[fwd][0], "gm", "oh", "r", lo)
    else:
        send(roles[back][2], "gp", "oh", "c", lo)
        send(roles[back][1], "gp", "oh", "p", lo)
    final = low
    g.tensor.wait_ge(S.tc, 4)
    for i in range(4):
        product(final[i], i, False)
    add(peers[0], final)
    add(peers[1], final)

    place = {X: 0, R: 1, Z: 2}[core]
    mine_of = {X: ("p", None), R: ("a", "p"), Z: ("b", "c")}[core]
    for part in ("qr" if core == X else mine_of[0]):
        g.wait_ge(S["gm" + part], count["g"])
    send(roles[fwd][place], "gd", "gm", mine_of[0], lo)
    spread("gm", mine_of[0])
    if mine_of[1]:
        g.wait_ge(S["gp" + mine_of[1]], count["g"])
        spread("gp", mine_of[1])
    g.wait_ge(S["gd" + mine_of[0]], count["g"])
    spread("gd", mine_of[0])

    add("gm", final)
    add("gp", final)
    add("gd", final, "fm")
    drain(T.yst, final, "fm", "yc")
    g.sync.wait_ge(S.yc, 4)
    g.sync.dma_start(T.y[:], T.yst[:]).then_inc(S.st, 16)
    g.sync.wait_ge(S.st, 16)
    g.wait_ge(S.sent, sent[0])
